import numpy as np, ml_dtypes
CORES = [10,34,74,98]
N = 4
KT, FB, TK = 1, 32, 256
def setup_inputs(rng):
    return {"x": rng.standard_normal((N, 128, KT * TK), dtype=np.float32).astype(ml_dtypes.bfloat16), "w": rng.standard_normal((N, 128, KT * N * FB), dtype=np.float32).astype(ml_dtypes.bfloat16)}
def setup_inputs_big(rng):
    d = setup_inputs(rng)
    for k in ("x", "w"): d[k] = (d[k].astype(np.float32) * 1024.0).astype(d[k].dtype)
    return d
def setup_inputs_small(rng):
    d = setup_inputs(rng)
    for k in ("x", "w"): d[k] = (d[k].astype(np.float32) * (1 / 1024.0)).astype(d[k].dtype)
    return d
def setup_inputs_apart(rng):
    d = setup_inputs(rng)
    f = (10.0 ** rng.permutation(np.linspace(-1.5, 1.5, N))).astype(np.float32).reshape(N, 1, 1)
    for k in ("x", "w"): d[k] = (d[k].astype(np.float32) * f).astype(d[k].dtype)
    return d
def reference(x, w):
    X, W = x.astype(np.float64), w.astype(np.float64)
    y = np.zeros((N, FB, N * TK))
    for j in range(N):
        for r in range(N):
            for t in range(KT):
                y[r][:, TK * j:TK * j + TK] += W[j][:, FB * (N * t + r):FB * (N * t + r) + FB].T @ X[j][:, TK * t:TK * t + TK]
    return {"y": y.astype(ml_dtypes.bfloat16 if x.dtype != np.float64 else np.float64)}

@@ -1,0 +1,138 @@
+from concourse.bass import DstId, RemoteDMATransfer
+
+N, FB, TK = 4, 32, 256
+Q = 128 // FB
+QC = TK // Q
+PAD = 8
+
+DIRECT = (1,)
+STAGED = (3, 2)
+
+SCRATCH = {
+    "xs": ("sbuf", [128, TK], "bfloat16"),
+    "ws": ("sbuf", [128, N * FB], "bfloat16"),
+    "wz": ("sbuf", [128, PAD + Q * N * FB], "bfloat16"),
+    "sp": ("sbuf", [128, TK], "bfloat16"),
+    "sa": ("sbuf", [128, QC * max(1, len(DIRECT))], "bfloat16"),
+    "pp": ("psum", [128, 512], "float32"),
+    "dout": ("dram", [max(1, len(STAGED)), 128, QC], "bfloat16"),
+    "din": ("dram", [N, 128, QC], "bfloat16"),
+}
+for _i in range(len(DIRECT)):
+    SCRATCH["pa%d" % _i] = ("psum", [128, 512], "float32")
+
+SEMAPHORES = (["lx", "lw", "zf", "wzr", "mmp", "cpp", "sent", "stored"]
+              + ["mma%d" % i for i in range(len(DIRECT))] + ["cpa%d" % i for i in range(len(DIRECT))]
+              + ["stg%d" % k for k in range(len(STAGED))] + ["arr%d" % s for s in range(N)])
+
+
+def _engines(topo, src, dst):
+    m = topo.mask(src, dst)
+    return [e for e in range(m.bit_length()) if (m >> e) & 1]
+
+
+def _bits(es):
+    v = 0
+    for e in es:
+        v |= 1 << e
+    return v
+
+
+def _share(n, k):
+    s = 1
+    while 2 * s * k <= n:
+        s *= 2
+    return s
+
+
+def _direct_engines(topo, src, dst):
+    return _engines(topo, src, dst)
+
+
+def _staged_engines(topo, src, dst, k):
+    es = _engines(topo, src, dst)
+    s = _share(len(es), len(STAGED))
+    return es[k * s:(k + 1) * s]
+
+
+def rank_program(g, core, T, topo):
+    j = T.rank_of(core)
+    if j is None:
+        return
+    sem, cores = T.sem, T.cores
+    for d in cores:
+        assert d == core or topo.may_write(core, d)
+    queues = [g.sync, g.scalar]
+
+    g.sync.dma_start(T.xs[:], T.x[:]).then_inc(sem.lx, 16)
+    g.scalar.dma_start(T.ws[:], T.w[:]).then_inc(sem.lw, 16)
+    if DIRECT:
+        g.vector.memset(T.wz[:], 0.0).then_inc(sem.zf, 1)
+        g.vector.wait_ge(sem.zf, 1)
+        g.vector.wait_ge(sem.lw, 16)
+        g.vector.tensor_copy(T.wz[:, PAD:PAD + Q * N * FB:Q], T.ws[:]).then_inc(sem.wzr, 1)
+
+    g.tensor.wait_ge(sem.lx, 16)
+    g.tensor.wait_ge(sem.lw, 16)
+    g.tensor.matmul(T.pp[:, 0:TK], T.ws[:], T.xs[:], start=True, stop=True).then_inc(sem.mmp, 1)
+    if DIRECT:
+        g.tensor.wait_ge(sem.zf, 1)
+        g.tensor.wait_ge(sem.wzr, 1)
+    for i, off in enumerate(DIRECT):
+        r = (j + off) % N
+        for q in range(Q):
+            lo = PAD + Q * FB * r - q
+            ins = g.tensor.matmul(T["pa%d" % i][:, 0:QC], T.wz[:, lo:lo + 128], T.xs[:, QC * q:QC * (q + 1)],
+                                  start=(q == 0), stop=(q == Q - 1))
+        ins.then_inc(sem["mma%d" % i], 1)
+
+    g.vector.wait_ge(sem.mmp, 1)
+    g.vector.tensor_copy(T.sp[:], T.pp[:, 0:TK]).then_inc(sem.cpp, 1)
+    for i in range(len(DIRECT)):
+        g.vector.wait_ge(sem["mma%d" % i], 1)
+        g.vector.tensor_copy(T.sa[:, QC * i:QC * (i + 1)], T["pa%d" % i][:, 0:QC]).then_inc(sem["cpa%d" % i], 1)
+
+    g.sync.wait_ge(sem.cpp, 1)
+    g.scalar.wait_ge(sem.cpp, 1)
+    for k, off in enumerate(STAGED):
+        r = (j + off) % N
+        queues[k % 2].dma_start(T.dout[k], T.sp[FB * r:FB * (r + 1), :]).then_inc(sem["stg%d" % k], 16)
+    queues[len(STAGED) % 2].dma_start(T.y[:, TK * j:TK * (j + 1)], T.sp[FB * j:FB * (j + 1), :]).then_inc(sem.stored, 16)
+
+    sent = 0
+    for i, off in enumerate(DIRECT):
+        dst = cores[(j + off) % N]
+        rid, pid, _ = topo.addr(dst)
+        es = _direct_engines(topo, core, dst)
+        g.wait_ge(sem["cpa%d" % i], 1)
+        g.remote_dma(out_ap=T.din[j], in_ap=T.sa[:, QC * i:QC * (i + 1)], remote_sem=sem["arr%d" % j],
+                     local_sem=sem.sent, pid=pid, routing_id=rid, dma_engine_mask=_bits(es))
+        sent += len(es)
+    if STAGED:
+        trs = []
+        for k, off in enumerate(STAGED):
+            dst = cores[(j + off) % N]
+            rid, pid, _ = topo.addr(dst)
+            es = _staged_engines(topo, core, dst, k)
+            g.wait_ge(sem["stg%d" % k], 16)
+            trs.append(RemoteDMATransfer(dst_ids=[DstId(rid=rid, pnc=pid)], dma_engine_mask=_bits(es),
+                                         remote_sem=sem["arr%d" % j], src=T.dout[k], dst=T.din[j]))
+            sent += len(es)
+        g.remote_dma_fused(trs, local_sem=sem.sent)
+
+    n = 0
+    for i, off in enumerate(DIRECT):
+        s = (j - off) % N
+        qd = queues[n % 2]
+        qd.wait_ge(sem["arr%d" % s], len(_direct_engines(topo, cores[s], core)))
+        qd.dma_start(T.y[:, TK * s:TK * (s + 1)], T.din[s]).then_inc(sem.stored, 16)
+        n += 1
+    for k, off in enumerate(STAGED):
+        s = (j - off) % N
+        qd = queues[n % 2]
+        qd.wait_ge(sem["arr%d" % s], len(_staged_engines(topo, cores[s], core, k)))
+        qd.dma_start(T.y[:, TK * s:TK * (s + 1)], T.din[s]).then_inc(sem.stored, 16)
+        n += 1
+
+    g.wait_ge(sem.sent, sent)
+    g.wait_ge(sem.stored, 16 * N)

@@ -1,58 +1,42 @@
-from concourse.bass import DstId, RemoteDMATransfer
-
 N, FB, TK = 4, 32, 256
 Q = 128 // FB
 QC = TK // Q
+RC = 16
+AC = (TK - RC) // Q
 PAD = 8
-
-DIRECT = (1,)
-STAGED = (3, 2)
+REG = PAD + 128
 
 SCRATCH = {
-    "xs": ("sbuf", [128, TK], "bfloat16"),
+    "bx": ("sbuf", [128, FB + TK], "bfloat16"),
     "ws": ("sbuf", [128, N * FB], "bfloat16"),
-    "wz": ("sbuf", [128, PAD + Q * N * FB], "bfloat16"),
-    "sp": ("sbuf", [128, TK], "bfloat16"),
-    "sa": ("sbuf", [128, QC * max(1, len(DIRECT))], "bfloat16"),
-    "pp": ("psum", [128, 512], "float32"),
-    "dout": ("dram", [max(1, len(STAGED)), 128, QC], "bfloat16"),
+    "wz": ("sbuf", [128, (N - 1) * REG], "bfloat16"),
+    "sa": ("sbuf", [128, (N - 1) * QC], "bfloat16"),
+    "so": ("sbuf", [128, TK], "bfloat16"),
+    "rin": ("sbuf", [128, FB + RC], "bfloat16"),
+    "sr": ("sbuf", [128, RC], "bfloat16"),
+    "po": ("psum", [128, 512], "float32"),
+    "pr": ("psum", [128, 512], "float32"),
+    "dina": ("dram", [128, AC], "bfloat16"),
     "din": ("dram", [N, 128, QC], "bfloat16"),
 }
-for _i in range(len(DIRECT)):
-    SCRATCH["pa%d" % _i] = ("psum", [128, 512], "float32")
+for _k in range(N - 1):
+    SCRATCH["pa%d" % _k] = ("psum", [128, 512], "float32")
 
-SEMAPHORES = (["lx", "lw", "zf", "wzr", "mmp", "cpp", "sent", "stored"]
-              + ["mma%d" % i for i in range(len(DIRECT))] + ["cpa%d" % i for i in range(len(DIRECT))]
-              + ["stg%d" % k for k in range(len(STAGED))] + ["arr%d" % s for s in range(N)])
-
-
-def _engines(topo, src, dst):
-    m = topo.mask(src, dst)
-    return [e for e in range(m.bit_length()) if (m >> e) & 1]
+SEMAPHORES = (["lr", "lx", "lw", "zf", "sp0", "sp1", "mmo", "cpo", "mmr", "cpr", "sent", "stored", "arw"]
+              + ["mm%d" % k for k in range(N - 1)] + ["cp%d" % k for k in range(N - 1)]
+              + ["arr%d" % k for k in range(N - 1)])
 
 
-def _bits(es):
-    v = 0
-    for e in es:
-        v |= 1 << e
-    return v
+def _order(topo, cores, s):
+    return sorted(range(1, N), key=lambda o: topo.same_plane(topo.chip(cores[s]), topo.chip(cores[(s + o) % N])))
 
 
-def _share(n, k):
-    s = 1
-    while 2 * s * k <= n:
-        s *= 2
-    return s
-
-
-def _direct_engines(topo, src, dst):
-    return _engines(topo, src, dst)
-
-
-def _staged_engines(topo, src, dst, k):
-    es = _engines(topo, src, dst)
-    s = _share(len(es), len(STAGED))
-    return es[k * s:(k + 1) * s]
+def _count(m):
+    n = 0
+    while m:
+        n += m & 1
+        m >>= 1
+    return n
 
 
 def rank_program(g, core, T, topo):
@@ -62,77 +46,90 @@ def rank_program(g, core, T, topo):
     sem, cores = T.sem, T.cores
     for d in cores:
         assert d == core or topo.may_write(core, d)
-    queues = [g.sync, g.scalar]
+    for k in range(N - 1):
+        assert len({(s + _order(topo, cores, s)[k]) % N for s in range(N)}) == N
+    dests = [(j + o) % N for o in _order(topo, cores, j)]
+    srcs = [[s for s in range(N) if s != j and (s + _order(topo, cores, s)[k]) % N == j][0] for k in range(N - 1)]
+    xs0 = FB
 
-    g.sync.dma_start(T.xs[:], T.x[:]).then_inc(sem.lx, 16)
+    g.sync.dma_start(T.bx[:, 0:FB], T.w[:, FB * dests[0]:FB * (dests[0] + 1)]).then_inc(sem.lr, 16)
+    g.scalar.dma_start(T.bx[:, xs0:xs0 + RC], T.x[:, 0:RC]).then_inc(sem.lr, 16)
+    g.sync.dma_start(T.bx[:, xs0 + RC:xs0 + TK], T.x[:, RC:TK]).then_inc(sem.lx, 16)
     g.scalar.dma_start(T.ws[:], T.w[:]).then_inc(sem.lw, 16)
-    if DIRECT:
-        g.vector.memset(T.wz[:], 0.0).then_inc(sem.zf, 1)
-        g.vector.wait_ge(sem.zf, 1)
-        g.vector.wait_ge(sem.lw, 16)
-        g.vector.tensor_copy(T.wz[:, PAD:PAD + Q * N * FB:Q], T.ws[:]).then_inc(sem.wzr, 1)
 
+    g.vector.memset(T.wz[:], 0.0).then_inc(sem.zf, 1)
+    g.vector.wait_ge(sem.zf, 1)
+    g.vector.wait_ge(sem.lr, 32)
+    g.vector.tensor_copy(T.wz[:, PAD:PAD + 128:Q], T.bx[:, 0:FB]).then_inc(sem.sp0, 1)
+    g.vector.wait_ge(sem.lw, 16)
+    for k in range(1, N - 1):
+        r = dests[k]
+        g.vector.tensor_copy(T.wz[:, REG * k + PAD:REG * k + PAD + 128:Q], T.ws[:, FB * r:FB * (r + 1)]).then_inc(sem.sp1, 1)
+
+    g.tensor.wait_ge(sem.zf, 1)
+    g.tensor.wait_ge(sem.sp0, 1)
+    g.tensor.wait_ge(sem.lr, 32)
     g.tensor.wait_ge(sem.lx, 16)
-    g.tensor.wait_ge(sem.lw, 16)
-    g.tensor.matmul(T.pp[:, 0:TK], T.ws[:], T.xs[:], start=True, stop=True).then_inc(sem.mmp, 1)
-    if DIRECT:
-        g.tensor.wait_ge(sem.zf, 1)
-        g.tensor.wait_ge(sem.wzr, 1)
-    for i, off in enumerate(DIRECT):
-        r = (j + off) % N
+    for k in range(N - 1):
+        c0 = RC if k == 0 else 0
+        wd = (TK - c0) // Q
+        if k == 1:
+            g.tensor.wait_ge(sem.sp1, N - 2)
         for q in range(Q):
-            lo = PAD + Q * FB * r - q
-            ins = g.tensor.matmul(T["pa%d" % i][:, 0:QC], T.wz[:, lo:lo + 128], T.xs[:, QC * q:QC * (q + 1)],
-                                  start=(q == 0), stop=(q == Q - 1))
-        ins.then_inc(sem["mma%d" % i], 1)
+            lo = REG * k + PAD - q
+            ins = g.tensor.matmul(T["pa%d" % k][:, 0:wd], T.wz[:, lo:lo + 128],
+                                  T.bx[:, xs0 + c0 + wd * q:xs0 + c0 + wd * (q + 1)], start=(q == 0), stop=(q == Q - 1))
+        ins.then_inc(sem["mm%d" % k], 1)
+    g.tensor.wait_ge(sem.lw, 16)
+    g.tensor.matmul(T.po[0:FB, 0:TK], T.ws[:, FB * j:FB * (j + 1)], T.bx[:, xs0:xs0 + TK],
+                    start=True, stop=True).then_inc(sem.mmo, 1)
+    g.tensor.wait_ge(sem.arw, _count(topo.mask(cores[srcs[0]], core)))
+    g.tensor.matmul(T.pr[0:FB, 0:RC], T.rin[:, 0:FB], T.rin[:, FB:FB + RC], start=True, stop=True).then_inc(sem.mmr, 1)
 
-    g.vector.wait_ge(sem.mmp, 1)
-    g.vector.tensor_copy(T.sp[:], T.pp[:, 0:TK]).then_inc(sem.cpp, 1)
-    for i in range(len(DIRECT)):
-        g.vector.wait_ge(sem["mma%d" % i], 1)
-        g.vector.tensor_copy(T.sa[:, QC * i:QC * (i + 1)], T["pa%d" % i][:, 0:QC]).then_inc(sem["cpa%d" % i], 1)
-
-    g.sync.wait_ge(sem.cpp, 1)
-    g.scalar.wait_ge(sem.cpp, 1)
-    for k, off in enumerate(STAGED):
-        r = (j + off) % N
-        queues[k % 2].dma_start(T.dout[k], T.sp[FB * r:FB * (r + 1), :]).then_inc(sem["stg%d" % k], 16)
-    queues[len(STAGED) % 2].dma_start(T.y[:, TK * j:TK * (j + 1)], T.sp[FB * j:FB * (j + 1), :]).then_inc(sem.stored, 16)
+    for k in range(N - 1):
+        wd = AC if k == 0 else QC
+        g.vector.wait_ge(sem["mm%d" % k], 1)
+        g.vector.tensor_copy(T.sa[:, QC * k:QC * k + wd], T["pa%d" % k][:, 0:wd]).then_inc(sem["cp%d" % k], 1)
+    g.vector.wait_ge(sem.mmo, 1)
+    g.vector.tensor_copy(T.so[0:FB, :], T.po[0:FB, 0:TK]).then_inc(sem.cpo, 1)
+    g.vector.wait_ge(sem.mmr, 1)
+    g.vector.tensor_copy(T.sr[0:FB, :], T.pr[0:FB, 0:RC]).then_inc(sem.cpr, 1)
 
     sent = 0
-    for i, off in enumerate(DIRECT):
-        dst = cores[(j + off) % N]
+    dst = cores[dests[0]]
+    rid, pid, _ = topo.addr(dst)
+    m = topo.mask(core, dst)
+    g.wait_ge(sem.lr, 32)
+    g.remote_dma(out_ap=T.rin[:], in_ap=T.bx[:, 0:FB + RC], remote_sem=sem.arw, local_sem=sem.sent,
+                 pid=pid, routing_id=rid, dma_engine_mask=m)
+    sent += _count(m)
+    for k in range(N - 1):
+        dst = cores[dests[k]]
         rid, pid, _ = topo.addr(dst)
-        es = _direct_engines(topo, core, dst)
-        g.wait_ge(sem["cpa%d" % i], 1)
-        g.remote_dma(out_ap=T.din[j], in_ap=T.sa[:, QC * i:QC * (i + 1)], remote_sem=sem["arr%d" % j],
-                     local_sem=sem.sent, pid=pid, routing_id=rid, dma_engine_mask=_bits(es))
-        sent += len(es)
-    if STAGED:
-        trs = []
-        for k, off in enumerate(STAGED):
-            dst = cores[(j + off) % N]
-            rid, pid, _ = topo.addr(dst)
-            es = _staged_engines(topo, core, dst, k)
-            g.wait_ge(sem["stg%d" % k], 16)
-            trs.append(RemoteDMATransfer(dst_ids=[DstId(rid=rid, pnc=pid)], dma_engine_mask=_bits(es),
-                                         remote_sem=sem["arr%d" % j], src=T.dout[k], dst=T.din[j]))
-            sent += len(es)
-        g.remote_dma_fused(trs, local_sem=sem.sent)
+        m = topo.mask(core, dst)
+        wd = AC if k == 0 else QC
+        g.wait_ge(sem["cp%d" % k], 1)
+        g.remote_dma(out_ap=(T.dina[:] if k == 0 else T.din[j]), in_ap=T.sa[:, QC * k:QC * k + wd],
+                     remote_sem=sem["arr%d" % k], local_sem=sem.sent, pid=pid, routing_id=rid, dma_engine_mask=m)
+        sent += _count(m)
 
-    n = 0
-    for i, off in enumerate(DIRECT):
-        s = (j - off) % N
-        qd = queues[n % 2]
-        qd.wait_ge(sem["arr%d" % s], len(_direct_engines(topo, cores[s], core)))
-        qd.dma_start(T.y[:, TK * s:TK * (s + 1)], T.din[s]).then_inc(sem.stored, 16)
-        n += 1
-    for k, off in enumerate(STAGED):
-        s = (j - off) % N
-        qd = queues[n % 2]
-        qd.wait_ge(sem["arr%d" % s], len(_staged_engines(topo, cores[s], core, k)))
-        qd.dma_start(T.y[:, TK * s:TK * (s + 1)], T.din[s]).then_inc(sem.stored, 16)
-        n += 1
+    def arrived(qd, k):
+        qd.wait_ge(sem["arr%d" % k], _count(topo.mask(cores[srcs[k]], core)))
+
+    s = srcs[0]
+    arrived(g.sync, 0)
+    g.sync.dma_start(T.y[:, TK * s + RC:TK * (s + 1)], T.dina[:]).then_inc(sem.stored, 16)
+    s = srcs[1]
+    arrived(g.scalar, 1)
+    g.scalar.dma_start(T.y[:, TK * s:TK * (s + 1)], T.din[s]).then_inc(sem.stored, 16)
+    g.scalar.wait_ge(sem.cpo, 1)
+    g.scalar.dma_start(T.y[:, TK * j:TK * (j + 1)], T.so[0:FB, :]).then_inc(sem.stored, 16)
+    g.scalar.wait_ge(sem.cpr, 1)
+    s = srcs[0]
+    g.scalar.dma_start(T.y[:, TK * s:TK * s + RC], T.sr[0:FB, :]).then_inc(sem.stored, 16)
+    s = srcs[2]
+    arrived(g.sync, 2)
+    g.sync.dma_start(T.y[:, TK * s:TK * (s + 1)], T.din[s]).then_inc(sem.stored, 16)
 
     g.wait_ge(sem.sent, sent)
-    g.wait_ge(sem.stored, 16 * N)
+    g.wait_ge(sem.stored, 16 * (N + 1))

N, FB, TK = 4, 32, 256
Q = 128 // FB
QC = TK // Q
RC = 16
AC = (TK - RC) // Q
PAD = 8
REG = PAD + 128

SCRATCH = {
    "bx": ("sbuf", [128, FB + TK], "bfloat16"),
    "ws": ("sbuf", [128, N * FB], "bfloat16"),
    "wz": ("sbuf", [128, (N - 1) * REG], "bfloat16"),
    "sa": ("sbuf", [128, (N - 1) * QC], "bfloat16"),
    "so": ("sbuf", [128, TK], "bfloat16"),
    "rin": ("sbuf", [128, FB + RC], "bfloat16"),
    "sr": ("sbuf", [128, RC], "bfloat16"),
    "po": ("psum", [128, 512], "float32"),
    "pr": ("psum", [128, 512], "float32"),
    "dina": ("dram", [128, AC], "bfloat16"),
    "din": ("dram", [N, 128, QC], "bfloat16"),
}
for _k in range(N - 1):
    SCRATCH["pa%d" % _k] = ("psum", [128, 512], "float32")

SEMAPHORES = (["lr", "lx", "lw", "zf", "sp0", "sp1", "mmo", "cpo", "mmr", "cpr", "sent", "stored", "arw"]
              + ["mm%d" % k for k in range(N - 1)] + ["cp%d" % k for k in range(N - 1)]
              + ["arr%d" % k for k in range(N - 1)])


def _order(topo, cores, s):
    return sorted(range(1, N), key=lambda o: topo.same_plane(topo.chip(cores[s]), topo.chip(cores[(s + o) % N])))


def _count(m):
    n = 0
    while m:
        n += m & 1
        m >>= 1
    return n


def rank_program(g, core, T, topo):
    j = T.rank_of(core)
    if j is None:
        return
    sem, cores = T.sem, T.cores
    for d in cores:
        assert d == core or topo.may_write(core, d)
    for k in range(N - 1):
        assert len({(s + _order(topo, cores, s)[k]) % N for s in range(N)}) == N
    dests = [(j + o) % N for o in _order(topo, cores, j)]
    srcs = [[s for s in range(N) if s != j and (s + _order(topo, cores, s)[k]) % N == j][0] for k in range(N - 1)]
    xs0 = FB

    g.sync.dma_start(T.bx[:, 0:FB], T.w[:, FB * dests[0]:FB * (dests[0] + 1)]).then_inc(sem.lr, 16)
    g.scalar.dma_start(T.bx[:, xs0:xs0 + RC], T.x[:, 0:RC]).then_inc(sem.lr, 16)
    g.sync.dma_start(T.bx[:, xs0 + RC:xs0 + TK], T.x[:, RC:TK]).then_inc(sem.lx, 16)
    g.scalar.dma_start(T.ws[:], T.w[:]).then_inc(sem.lw, 16)

    g.vector.memset(T.wz[:], 0.0).then_inc(sem.zf, 1)
    g.vector.wait_ge(sem.zf, 1)
    g.vector.wait_ge(sem.lr, 32)
    g.vector.tensor_copy(T.wz[:, PAD:PAD + 128:Q], T.bx[:, 0:FB]).then_inc(sem.sp0, 1)
    g.vector.wait_ge(sem.lw, 16)
    for k in range(1, N - 1):
        r = dests[k]
        g.vector.tensor_copy(T.wz[:, REG * k + PAD:REG * k + PAD + 128:Q], T.ws[:, FB * r:FB * (r + 1)]).then_inc(sem.sp1, 1)

    g.tensor.wait_ge(sem.zf, 1)
    g.tensor.wait_ge(sem.sp0, 1)
    g.tensor.wait_ge(sem.lr, 32)
    g.tensor.wait_ge(sem.lx, 16)
    for k in range(N - 1):
        c0 = RC if k == 0 else 0
        wd = (TK - c0) // Q
        if k == 1:
            g.tensor.wait_ge(sem.sp1, N - 2)
        for q in range(Q):
            lo = REG * k + PAD - q
            ins = g.tensor.matmul(T["pa%d" % k][:, 0:wd], T.wz[:, lo:lo + 128],
                                  T.bx[:, xs0 + c0 + wd * q:xs0 + c0 + wd * (q + 1)], start=(q == 0), stop=(q == Q - 1))
        ins.then_inc(sem["mm%d" % k], 1)
    g.tensor.wait_ge(sem.lw, 16)
    g.tensor.matmul(T.po[0:FB, 0:TK], T.ws[:, FB * j:FB * (j + 1)], T.bx[:, xs0:xs0 + TK],
                    start=True, stop=True).then_inc(sem.mmo, 1)
    g.tensor.wait_ge(sem.arw, _count(topo.mask(cores[srcs[0]], core)))
    g.tensor.matmul(T.pr[0:FB, 0:RC], T.rin[:, 0:FB], T.rin[:, FB:FB + RC], start=True, stop=True).then_inc(sem.mmr, 1)

    for k in range(N - 1):
        wd = AC if k == 0 else QC
        g.vector.wait_ge(sem["mm%d" % k], 1)
        g.vector.tensor_copy(T.sa[:, QC * k:QC * k + wd], T["pa%d" % k][:, 0:wd]).then_inc(sem["cp%d" % k], 1)
    g.vector.wait_ge(sem.mmo, 1)
    g.vector.tensor_copy(T.so[0:FB, :], T.po[0:FB, 0:TK]).then_inc(sem.cpo, 1)
    g.vector.wait_ge(sem.mmr, 1)
    g.vector.tensor_copy(T.sr[0:FB, :], T.pr[0:FB, 0:RC]).then_inc(sem.cpr, 1)

    sent = 0
    dst = cores[dests[0]]
    rid, pid, _ = topo.addr(dst)
    m = topo.mask(core, dst)
    g.wait_ge(sem.lr, 32)
    g.remote_dma(out_ap=T.rin[:], in_ap=T.bx[:, 0:FB + RC], remote_sem=sem.arw, local_sem=sem.sent,
                 pid=pid, routing_id=rid, dma_engine_mask=m)
    sent += _count(m)
    for k in range(N - 1):
        dst = cores[dests[k]]
        rid, pid, _ = topo.addr(dst)
        m = topo.mask(core, dst)
        wd = AC if k == 0 else QC
        g.wait_ge(sem["cp%d" % k], 1)
        g.remote_dma(out_ap=(T.dina[:] if k == 0 else T.din[j]), in_ap=T.sa[:, QC * k:QC * k + wd],
                     remote_sem=sem["arr%d" % k], local_sem=sem.sent, pid=pid, routing_id=rid, dma_engine_mask=m)
        sent += _count(m)

    def arrived(qd, k):
        qd.wait_ge(sem["arr%d" % k], _count(topo.mask(cores[srcs[k]], core)))

    s = srcs[0]
    arrived(g.sync, 0)
    g.sync.dma_start(T.y[:, TK * s + RC:TK * (s + 1)], T.dina[:]).then_inc(sem.stored, 16)
    s = srcs[1]
    arrived(g.scalar, 1)
    g.scalar.dma_start(T.y[:, TK * s:TK * (s + 1)], T.din[s]).then_inc(sem.stored, 16)
    g.scalar.wait_ge(sem.cpo, 1)
    g.scalar.dma_start(T.y[:, TK * j:TK * (j + 1)], T.so[0:FB, :]).then_inc(sem.stored, 16)
    g.scalar.wait_ge(sem.cpr, 1)
    s = srcs[0]
    g.scalar.dma_start(T.y[:, TK * s:TK * s + RC], T.sr[0:FB, :]).then_inc(sem.stored, 16)
    s = srcs[2]
    arrived(g.sync, 2)
    g.sync.dma_start(T.y[:, TK * s:TK * (s + 1)], T.din[s]).then_inc(sem.stored, 16)

    g.wait_ge(sem.sent, sent)
    g.wait_ge(sem.stored, 16 * (N + 1))
